import numpy as np
import ml_dtypes


def mxq(x, axis, fmt="e4m3"):
    dtype, down = {"e4m3": (ml_dtypes.float8_e4m3fn, 7), "e5m2": (ml_dtypes.float8_e5m2, 14)}[fmt]
    v = np.moveaxis(np.asarray(x, np.float32).astype(ml_dtypes.bfloat16).astype(np.float64), axis, -1)
    blocks = v.reshape(v.shape[:-1] + (-1, 32))
    amax = np.abs(blocks).max(-1, keepdims=True)
    byte = np.maximum(np.where(amax > 0, np.frexp(amax)[1] - 1 + 127, 0) - down, 1)
    scale = np.exp2(byte - 127.0)
    codes = (blocks / scale).astype(np.float32).astype(dtype).astype(np.float64)
    return np.moveaxis((codes * scale).reshape(v.shape), -1, axis)


WIDE = False


def mx_kscale(k):
    if not WIDE:
        return np.ones(k)
    levels = np.array([10, -10, 5, -5, 0])
    if k % 512:
        return np.exp2(np.random.permutation(np.resize(levels, k // 32))).repeat(32)
    a = np.empty((k // 512, 16))
    for p in range(k // 512):
        a[p, :8] = np.random.permutation(np.resize(levels, 8))
        for g in range(8):
            far = levels[np.abs(levels - a[p, g]) >= 10]
            a[p, g + 8] = far[np.random.randint(len(far))]
    return np.exp2(a.ravel()).repeat(32)


def f64(x):
    return np.asarray(x).astype(np.float64)


def striped(idx):
    return np.tile(np.asarray(idx).reshape(-1, 16).T, (8, 1)).astype(np.uint16)


def unstriped(offs):
    return offs[:16].T.reshape(-1).astype(np.int64)


E2M1 = np.array([0.0, 0.5, 1.0, 1.5, 2.0, 3.0, 4.0, 6.0, -0.0, -0.5, -1.0, -1.5, -2.0, -3.0, -4.0, -6.0])


def pack_weight(w, fmt):
    k, n = w.shape
    w = f64(np.asarray(w, np.float32).astype(ml_dtypes.bfloat16)).reshape(k // 32, 32, n)
    amax = np.abs(w).max(1)
    if fmt == "e4m3":
        byte = np.frexp(amax)[1] - 1 + 127 - 7
    else:
        mant, ex = np.frexp(amax / 6.0)
        byte = np.where(mant > 0.5, ex, ex - 1) + 127
    byte = np.clip(np.where(amax > 0, byte, 1), 1, 254)
    scaled = (w * np.exp2(127.0 - byte)[:, None, :]).reshape(k, n).astype(np.float32)
    by_word = np.ascontiguousarray(scaled.reshape(k // 512, 128, 4, n).transpose(0, 1, 3, 2))
    if fmt == "e4m3":
        words = by_word.astype(ml_dtypes.float8_e4m3fn).view(np.uint8)
    else:
        c = by_word.astype(ml_dtypes.float4_e2m1fn).view(np.uint8) & 0xF
        words = (c[..., 0::2] | (c[..., 1::2] << 4)).reshape(k // 512, 128, 2 * n)
    return np.ascontiguousarray(words), np.ascontiguousarray(byte.astype(np.uint8).reshape(k // 512, 16, n))


def unpack_weight(words, scales, fmt):
    g, _, n = scales.shape
    words = np.ascontiguousarray(words).reshape(g, 128, n, -1)
    if fmt == "e4m3":
        vals = words.view(ml_dtypes.float8_e4m3fn).astype(np.float64)
    else:
        nib = np.empty((g, 128, n, 4), np.uint8)
        nib[..., 0::2] = words & 0xF
        nib[..., 1::2] = words >> 4
        vals = E2M1[nib]
    vals = vals * np.repeat(np.exp2(scales.astype(np.float64) - 127.0), 8, axis=1)[..., None]
    return vals.transpose(0, 1, 3, 2).reshape(g * 512, n)


B, N, T, D, DV, NQ = 1, 512, 1024, 512, 128, 256


def setup_inputs():
    n = np.random.standard_normal
    idx = np.random.permutation(T)[:B * N]
    s = mx_kscale(D)[:, None]
    u = np.ones(T)
    u[idx] = mx_kscale(B * N)
    r = np.random.uniform(0.5, 2.0, T)
    qp = [pack_weight(x, "e4m3") for x in n((B, D, NQ)) * s * (1.00 / np.sqrt(D))]
    k = n((D, T)) / s
    v = n((DV, T)) / (u * r)
    kp = pack_weight(k, "e4m3")
    return {
        "q_words": np.stack([x[0] for x in qp]),
        "q_scales": np.stack([x[1] for x in qp]),
        "k_words": kp[0],
        "k_scales": kp[1],
        "vT": v.astype(np.float32),
        "vs": np.tile(u * r, (128, 1)).astype(np.float32),
        "kb": np.tile(n(T), (128, 1)).astype(np.float32),
        "offs": striped(idx),
    }


def reference(q_words, q_scales, k_words, k_scales, vT, vs, kb, offs):
    idx = unstriped(offs)
    k = unpack_weight(k_words, k_scales, "e4m3")
    v = f64(vT)
    pick = lambda x: x[:, idx].reshape(x.shape[0], B, N).transpose(1, 0, 2)
    q = np.stack([unpack_weight(q_words[b], q_scales[b], "e4m3") for b in range(B)])
    score = q.transpose(0, 2, 1) @ pick(k)
    score = score + pick(f64(kb))[:, :1, :]
    p = score / (1.0 + np.exp(-score))
    w = p * pick(f64(vs))[:, :1, :]
    y = mxq(w, 2, "e4m3") @ mxq(pick(v).transpose(0, 2, 1), 1, "e4m3")
    y = y / 16.0
    return y

@@ -1,0 +1,148 @@
+from contextlib import ExitStack
+
+import concourse.mybir as mybir
+from concourse.masks import make_identity
+
+F32 = mybir.dt.float32
+BF16 = mybir.dt.bfloat16
+I32 = mybir.dt.int32
+U32 = mybir.dt.uint32
+U16 = mybir.dt.uint16
+U8 = mybir.dt.uint8
+FP8X4 = mybir.dt.float8_e4m3fn_x4
+ACT = mybir.ActivationFunctionType
+ALU = mybir.AluOpType
+
+P = 128
+PACK = 4
+RUN = 8
+T, N, NQ, D, DV = 1024, 512, 256, 512, 128
+FLOPS = 2 * D * N * NQ + 2 * N * NQ * DV
+LIVE = 96
+
+
+def by_place(tile):
+    return tile.rearrange("p (t g r) -> p g t r", t=PACK, r=RUN)
+
+
+def tile_attend_silu_kb_topkq256n512t1024_kernel(tc, q_words, q_scales, k_words, k_scales, vT, vs, kb, offs, out):
+    nc = tc.nc
+    with ExitStack() as ctx:
+        sb = ctx.enter_context(tc.tile_pool(name="sb", bufs=1))
+        ps = ctx.enter_context(tc.psum_pool(name="ps", bufs=1))
+
+        offsets = sb.tile([P, N // 16], U16)
+        kb_pool = sb.tile([P, T], F32)
+        vs_pool = sb.tile([P, T], F32)
+        ks_pool = sb.tile([P, T], U8, align_bytes=64)
+        kw_pool = sb.tile([P, T], I32, align_bytes=64)
+        v_pool = sb.tile([P, T], F32)
+        qw = sb.tile([P, NQ], I32, align_bytes=64)
+        qs = sb.tile([P, NQ], U8, align_bytes=64)
+
+        nc.vector.memset(ks_pool[:].bitcast(I32), 0)
+        warm = sb.tile([P, 8], F32)
+        nc.vector.memset(warm[:], 0.0)
+        nc.vector.memset(qs[:].bitcast(I32), 0)
+        nc.vector.memset(kb_pool[0:LIVE, :], 0.0)
+        nc.vector.memset(vs_pool[:], 0.0)
+        warm_out = sb.tile([P, 8], F32)
+        nc.scalar.activation(warm_out[:], warm[:], ACT.Silu)
+
+        nc.sync.dma_start(offsets[:], offs)
+        nc.sync.dma_start(kb_pool[LIVE:P, :], kb[LIVE:P, :])
+        for Q in range(4):
+            nc.sync.dma_start(ks_pool[32 * Q : 32 * Q + 4, :].bitcast(I32), k_scales[0, 4 * Q : 4 * Q + 4, :].bitcast(I32))
+        nc.sync.dma_start(v_pool[:], vT)
+        nc.sync.dma_start(kw_pool[:], k_words[0].rearrange("p n r -> p (n r)").bitcast(I32))
+        nc.sync.dma_start(qw[:], q_words[0, 0].rearrange("p n r -> p (n r)").bitcast(I32))
+        for Q in range(4):
+            nc.sync.dma_start(qs[32 * Q : 32 * Q + 4, :].bitcast(I32), q_scales[0, 0, 4 * Q : 4 * Q + 4, :].bitcast(I32))
+        nc.sync.dma_start(vs_pool[0:1, :], vs[0:1, :])
+
+        ident32 = sb.tile([P, P], F32)
+        make_identity(nc, ident32[:])
+
+        kb_g = sb.tile([P, N], F32)
+        nc.vector.tensor_copy(by_place(kb_g[:].bitcast(U32)), kb_pool[:].bitcast(U32).indirect(offsets[:]))
+        ks_g = sb.tile([P, N], U8, align_bytes=64)
+        nc.vector.tensor_copy(ks_g[:], ks_pool[:].indirect(offsets[:]))
+        ks_p = sb.tile([P, N], U8, align_bytes=64)
+        nc.vector.tensor_copy(
+            ks_p[:].bitcast(I32).rearrange("p (t g w) -> p t g w", t=PACK, w=RUN // 4),
+            ks_g[:].bitcast(I32).rearrange("p (g t w) -> p t g w", t=PACK, w=RUN // 4),
+        )
+        kw_g = sb.tile([P, N], U32, align_bytes=64)
+        nc.vector.tensor_copy(by_place(kw_g[:]), kw_pool[:].bitcast(U32).indirect(offsets[:]))
+        vs_g = sb.tile([P, N], F32)
+        nc.vector.tensor_copy(by_place(vs_g[:].bitcast(U32)), vs_pool[:].bitcast(U32).indirect(offsets[:]))
+
+        v_bf = sb.tile([P, T], BF16)
+        nc.scalar.activation(v_bf[:], v_pool[:], ACT.Copy)
+        v_g = sb.tile([P, N], BF16)
+        nc.scalar.activation(v_g[:].rearrange("p (g r t) -> p g t r", t=PACK, r=RUN), v_bf[:].indirect(offsets[:]), ACT.Copy)
+
+        kb_t = ps.tile([P, PACK, P], F32, tag="first")
+        for t in range(PACK):
+            nc.tensor.transpose(kb_t[:, t, :], kb_g[:, t * P : (t + 1) * P], ident32[:])
+        kb_col = sb.tile([P, PACK], F32)
+        nc.scalar.copy(kb_col[:], kb_t[:, :, LIVE])
+
+        p_t = sb.tile([P, PACK, NQ], F32)
+        for t in range(PACK):
+            score = ps.tile([P, NQ], F32, name="score%d" % t, tag="score%d" % t)
+            cols = slice(t * P, (t + 1) * P)
+            nc.tensor.matmul_mx(
+                out=score[:],
+                lhsT=kw_g[:, cols].bitcast(FP8X4),
+                lhsT_scale=ks_p[:, cols],
+                rhs=qw[:].bitcast(FP8X4),
+                rhs_scale=qs[:],
+                start=True,
+                stop=True,
+            )
+            nc.scalar.activation(p_t[:, t, :], score[:], ACT.Silu, bias=kb_col[:, t : t + 1])
+
+        vs_t = ps.tile([P, PACK, P], F32)
+        for t in range(PACK):
+            nc.tensor.transpose(vs_t[:, t, :], vs_g[:, t * P : (t + 1) * P], ident32[:])
+
+        v_t = ps.tile([P, 2, P], F32, tag="score%d" % (PACK - 1))
+        v_pairs = v_g[:].bitcast(F32)
+        for u in range(2):
+            nc.tensor.transpose(v_t[:, u, :], v_pairs[:, u : 2 * P : 2], ident32[:])
+        v_in = sb.tile([P, DV * PACK], BF16, align_bytes=64)
+        nc.scalar.copy(v_in[:].bitcast(F32).rearrange("p (e u) -> p e u", u=2), v_t[:].rearrange("p u e -> p e u"))
+
+        halves = NQ // P
+        vs_col = vs_t[:, :, 0:1].rearrange("p t o -> p o t").to_broadcast([P, P, PACK])
+        w_in = [sb.tile([P, P, PACK], BF16, name="w_in%d" % h, align_bytes=64) for h in range(halves)]
+        for h in range(halves):
+            nc.vector.tensor_tensor(w_in[h][:], p_t[:, :, h * P : (h + 1) * P].rearrange("p t q -> p q t"), vs_col, ALU.mult)
+
+        v_codes = sb.tile([P, DV], U32, align_bytes=64)
+        v_scales = sb.tile([P, DV], U8, align_bytes=64)
+
+        for h in range(halves):
+            w_codes = sb.tile([P, P], U32, name="w_codes%d" % h, align_bytes=64)
+            w_scales = sb.tile([P, P], U8, name="w_scales%d" % h, align_bytes=64)
+            nc.vector.quantize_mx(out=w_codes[:].bitcast(FP8X4), scales=w_scales[:], in_=w_in[h][:].rearrange("p q t -> p (q t)"))
+            if h == 0:
+                nc.vector.quantize_mx(out=v_codes[:].bitcast(FP8X4), scales=v_scales[:], in_=v_in[:])
+            y = ps.tile([P, DV], F32, name="y%d" % h, tag=("second", "first")[h])
+            nc.tensor.matmul_mx(
+                out=y[:],
+                lhsT=w_codes[:].bitcast(FP8X4),
+                lhsT_scale=w_scales[:],
+                rhs=v_codes[:].bitcast(FP8X4),
+                rhs_scale=v_scales[:],
+                start=True,
+                stop=True,
+            )
+            res = sb.tile([P, DV], F32, name="res%d" % h)
+            if h == 0:
+                nc.scalar.activation(res[:], y[:], ACT.Copy, scale=1.0 / 16.0)
+                nc.scalar.dma_start(out[0, h * P : (h + 1) * P, :], res[:])
+            else:
+                nc.vector.tensor_scalar(res[:], y[:], 1.0 / 16.0, None, ALU.mult)
+                nc.sync.dma_start(out[0, h * P : (h + 1) * P, :], res[:])

@@ -16,9 +16,9 @@ ALU = mybir.AluOpType
 P = 128
 PACK = 4
 RUN = 8
+LIVE = 96
 T, N, NQ, D, DV = 1024, 512, 256, 512, 128
 FLOPS = 2 * D * N * NQ + 2 * N * NQ * DV
-LIVE = 96
 
 
 def by_place(tile):
@@ -40,33 +40,34 @@ def tile_attend_silu_kb_topkq256n512t1024_kernel(tc, q_words, q_scales, k_words,
         qw = sb.tile([P, NQ], I32, align_bytes=64)
         qs = sb.tile([P, NQ], U8, align_bytes=64)
 
-        nc.vector.memset(ks_pool[:].bitcast(I32), 0)
         warm = sb.tile([P, 8], F32)
         nc.vector.memset(warm[:], 0.0)
-        nc.vector.memset(qs[:].bitcast(I32), 0)
         nc.vector.memset(kb_pool[0:LIVE, :], 0.0)
-        nc.vector.memset(vs_pool[:], 0.0)
-        warm_out = sb.tile([P, 8], F32)
-        nc.scalar.activation(warm_out[:], warm[:], ACT.Silu)
-
-        nc.sync.dma_start(offsets[:], offs)
-        nc.sync.dma_start(kb_pool[LIVE:P, :], kb[LIVE:P, :])
-        for Q in range(4):
-            nc.sync.dma_start(ks_pool[32 * Q : 32 * Q + 4, :].bitcast(I32), k_scales[0, 4 * Q : 4 * Q + 4, :].bitcast(I32))
-        nc.sync.dma_start(v_pool[:], vT)
-        nc.sync.dma_start(kw_pool[:], k_words[0].rearrange("p n r -> p (n r)").bitcast(I32))
-        nc.sync.dma_start(qw[:], q_words[0, 0].rearrange("p n r -> p (n r)").bitcast(I32))
-        for Q in range(4):
-            nc.sync.dma_start(qs[32 * Q : 32 * Q + 4, :].bitcast(I32), q_scales[0, 0, 4 * Q : 4 * Q + 4, :].bitcast(I32))
-        nc.sync.dma_start(vs_pool[0:1, :], vs[0:1, :])
-
+        nc.vector.memset(vs_pool[0:LIVE, :], 0.0)
+        nc.vector.memset(qs[:].bitcast(I32), 0)
         ident32 = sb.tile([P, P], F32)
         make_identity(nc, ident32[:])
+
+        nc.scalar.dma_start(kb_pool[LIVE:P, :], kb[LIVE:P, :])
+        nc.sync.dma_start(offsets[:], offs)
+        for Q in range(4):
+            rows = k_scales[0, 4 * Q : 4 * Q + 4, :].bitcast(I32).unsqueeze(0).to_broadcast([8, 4, T // 4])
+            nc.sync.dma_start(ks_pool[32 * Q : 32 * Q + 32, :].bitcast(I32), rows)
+        nc.sync.dma_start(v_pool[:], vT)
+        nc.sync.dma_start(vs_pool[LIVE:P, :], vs[LIVE:P, :])
+        nc.sync.dma_start(kw_pool[:], k_words[0].rearrange("p n r -> p (n r)").bitcast(I32))
+        nc.sync.dma_start(qw[:], q_words[0, 0].rearrange("p n r -> p (n r)").bitcast(I32))
+        warm_out = sb.tile([P, 8], F32)
+        nc.scalar.activation(warm_out[:], warm[:], ACT.Silu)
+        for Q in range(4):
+            nc.sync.dma_start(qs[32 * Q : 32 * Q + 4, :].bitcast(I32), q_scales[0, 0, 4 * Q : 4 * Q + 4, :].bitcast(I32))
 
         kb_g = sb.tile([P, N], F32)
         nc.vector.tensor_copy(by_place(kb_g[:].bitcast(U32)), kb_pool[:].bitcast(U32).indirect(offsets[:]))
         ks_g = sb.tile([P, N], U8, align_bytes=64)
         nc.vector.tensor_copy(ks_g[:], ks_pool[:].indirect(offsets[:]))
+        vs_g = sb.tile([P, N], F32)
+        nc.vector.tensor_copy(by_place(vs_g[:].bitcast(U32)), vs_pool[:].bitcast(U32).indirect(offsets[:]))
         ks_p = sb.tile([P, N], U8, align_bytes=64)
         nc.vector.tensor_copy(
             ks_p[:].bitcast(I32).rearrange("p (t g w) -> p t g w", t=PACK, w=RUN // 4),
@@ -74,62 +75,69 @@ def tile_attend_silu_kb_topkq256n512t1024_kernel(tc, q_words, q_scales, k_words,
         )
         kw_g = sb.tile([P, N], U32, align_bytes=64)
         nc.vector.tensor_copy(by_place(kw_g[:]), kw_pool[:].bitcast(U32).indirect(offsets[:]))
-        vs_g = sb.tile([P, N], F32)
-        nc.vector.tensor_copy(by_place(vs_g[:].bitcast(U32)), vs_pool[:].bitcast(U32).indirect(offsets[:]))
 
         v_bf = sb.tile([P, T], BF16)
         nc.scalar.activation(v_bf[:], v_pool[:], ACT.Copy)
         v_g = sb.tile([P, N], BF16)
         nc.scalar.activation(v_g[:].rearrange("p (g r t) -> p g t r", t=PACK, r=RUN), v_bf[:].indirect(offsets[:]), ACT.Copy)
 
-        kb_t = ps.tile([P, PACK, P], F32, tag="first")
+        kb_t = ps.tile([P, PACK, P], F32, tag="bank4")
         for t in range(PACK):
             nc.tensor.transpose(kb_t[:, t, :], kb_g[:, t * P : (t + 1) * P], ident32[:])
         kb_col = sb.tile([P, PACK], F32)
         nc.scalar.copy(kb_col[:], kb_t[:, :, LIVE])
 
-        p_t = sb.tile([P, PACK, NQ], F32)
-        for t in range(PACK):
-            score = ps.tile([P, NQ], F32, name="score%d" % t, tag="score%d" % t)
-            cols = slice(t * P, (t + 1) * P)
-            nc.tensor.matmul_mx(
-                out=score[:],
-                lhsT=kw_g[:, cols].bitcast(FP8X4),
-                lhsT_scale=ks_p[:, cols],
-                rhs=qw[:].bitcast(FP8X4),
-                rhs_scale=qs[:],
-                start=True,
-                stop=True,
-            )
-            nc.scalar.activation(p_t[:, t, :], score[:], ACT.Silu, bias=kb_col[:, t : t + 1])
-
-        vs_t = ps.tile([P, PACK, P], F32)
+        vs_t = ps.tile([P, PACK, P], F32, tag="bank7")
         for t in range(PACK):
             nc.tensor.transpose(vs_t[:, t, :], vs_g[:, t * P : (t + 1) * P], ident32[:])
 
-        v_t = ps.tile([P, 2, P], F32, tag="score%d" % (PACK - 1))
+        v_t = ps.tile([P, 2, P], F32, tag="bank5")
         v_pairs = v_g[:].bitcast(F32)
         for u in range(2):
             nc.tensor.transpose(v_t[:, u, :], v_pairs[:, u : 2 * P : 2], ident32[:])
         v_in = sb.tile([P, DV * PACK], BF16, align_bytes=64)
         nc.scalar.copy(v_in[:].bitcast(F32).rearrange("p (e u) -> p e u", u=2), v_t[:].rearrange("p u e -> p e u"))
-
-        halves = NQ // P
-        vs_col = vs_t[:, :, 0:1].rearrange("p t o -> p o t").to_broadcast([P, P, PACK])
-        w_in = [sb.tile([P, P, PACK], BF16, name="w_in%d" % h, align_bytes=64) for h in range(halves)]
-        for h in range(halves):
-            nc.vector.tensor_tensor(w_in[h][:], p_t[:, :, h * P : (h + 1) * P].rearrange("p t q -> p q t"), vs_col, ALU.mult)
-
         v_codes = sb.tile([P, DV], U32, align_bytes=64)
         v_scales = sb.tile([P, DV], U8, align_bytes=64)
+        nc.vector.quantize_mx(out=v_codes[:].bitcast(FP8X4), scales=v_scales[:], in_=v_in[:])
+
+        halves = NQ // P
+        vs_col = vs_t[:, :, LIVE : LIVE + 1].unsqueeze(1).to_broadcast([P, P // 4, PACK, 4])
+        p_t = sb.tile([P, PACK, NQ], F32)
+
+        def weigh(t, queries, bank):
+            score = ps.tile([P, queries.stop - queries.start], F32, name="score", tag="bank%d" % bank)
+            cols = slice(t * P, (t + 1) * P)
+            nc.tensor.matmul_mx(
+                out=score[:],
+                lhsT=kw_g[:, cols].bitcast(FP8X4),
+                lhsT_scale=ks_p[:, cols],
+                rhs=qw[:, queries].bitcast(FP8X4),
+                rhs_scale=qs[:, queries],
+                start=True,
+                stop=True,
+            )
+            nc.scalar.activation(p_t[:, t, queries], score[:], ACT.Silu, bias=kb_col[:, t : t + 1])
+
+        w_in = []
+        for h in range(halves):
+            queries = slice(h * P, (h + 1) * P)
+            for t in range(PACK):
+                weigh(t, queries, (PACK * h + t) % 7)
+            w_h = sb.tile([P, P, PACK], BF16, name="w_in%d" % h, align_bytes=64)
+            nc.vector.tensor_tensor(
+                w_h[:].rearrange("p (c i) t -> p c t i", i=4),
+                p_t[:, :, queries].rearrange("p t (c i) -> p c t i", i=4),
+                vs_col,
+                ALU.mult,
+            )
+            w_in.append(w_h)
 
         for h in range(halves):
             w_codes = sb.tile([P, P], U32, name="w_codes%d" % h, align_bytes=64)
             w_scales = sb.tile([P, P], U8, name="w_scales%d" % h, align_bytes=64)
             nc.vector.quantize_mx(out=w_codes[:].bitcast(FP8X4), scales=w_scales[:], in_=w_in[h][:].rearrange("p q t -> p (q t)"))
-            if h == 0:
-                nc.vector.quantize_mx(out=v_codes[:].bitcast(FP8X4), scales=v_scales[:], in_=v_in[:])
-            y = ps.tile([P, DV], F32, name="y%d" % h, tag=("second", "first")[h])
+            y = ps.tile([P, DV], F32, name="y%d" % h, tag="bank%d" % (h + 1))
             nc.tensor.matmul_mx(
                 out=y[:],
                 lhsT=w_codes[:].bitcast(FP8X4),

@@ -102,7 +102,7 @@ def tile_attend_silu_kb_topkq256n512t1024_kernel(tc, q_words, q_scales, k_words,
         nc.vector.quantize_mx(out=v_codes[:].bitcast(FP8X4), scales=v_scales[:], in_=v_in[:])
 
         halves = NQ // P
-        vs_col = vs_t[:, :, LIVE : LIVE + 1].unsqueeze(1).to_broadcast([P, P // 4, PACK, 4])
+        vs_col = vs_t[:, :, LIVE : LIVE + 1].unsqueeze(1).to_broadcast([P, P // 2, PACK, 2])
         p_t = sb.tile([P, PACK, NQ], F32)
 
         def weigh(t, queries, bank):
@@ -126,8 +126,8 @@ def tile_attend_silu_kb_topkq256n512t1024_kernel(tc, q_words, q_scales, k_words,
                 weigh(t, queries, (PACK * h + t) % 7)
             w_h = sb.tile([P, P, PACK], BF16, name="w_in%d" % h, align_bytes=64)
             nc.vector.tensor_tensor(
-                w_h[:].rearrange("p (c i) t -> p c t i", i=4),
-                p_t[:, :, queries].rearrange("p t (c i) -> p c t i", i=4),
+                w_h[:].rearrange("p (c i) t -> p c t i", i=2),
+                p_t[:, :, queries].rearrange("p t (c i) -> p c t i", i=2),
                 vs_col,
                 ALU.mult,
             )

@@ -16,7 +16,7 @@ ALU = mybir.AluOpType
 P = 128
 PACK = 4
 RUN = 8
-LIVE = 96
+LIVE = 127
 T, N, NQ, D, DV = 1024, 512, 256, 512, 128
 FLOPS = 2 * D * N * NQ + 2 * N * NQ * DV
 

@@ -53,10 +53,10 @@ def tile_attend_silu_kb_topkq256n512t1024_kernel(tc, q_words, q_scales, k_words,
         for Q in range(4):
             rows = k_scales[0, 4 * Q : 4 * Q + 4, :].bitcast(I32).unsqueeze(0).to_broadcast([8, 4, T // 4])
             nc.sync.dma_start(ks_pool[32 * Q : 32 * Q + 32, :].bitcast(I32), rows)
-        nc.sync.dma_start(v_pool[:], vT)
-        nc.sync.dma_start(vs_pool[LIVE:P, :], vs[LIVE:P, :])
         nc.sync.dma_start(kw_pool[:], k_words[0].rearrange("p n r -> p (n r)").bitcast(I32))
         nc.sync.dma_start(qw[:], q_words[0, 0].rearrange("p n r -> p (n r)").bitcast(I32))
+        nc.sync.dma_start(vs_pool[LIVE:P, :], vs[LIVE:P, :])
+        nc.sync.dma_start(v_pool[:], vT)
         warm_out = sb.tile([P, 8], F32)
         nc.scalar.activation(warm_out[:], warm[:], ACT.Silu)
         for Q in range(4):
@@ -66,8 +66,6 @@ def tile_attend_silu_kb_topkq256n512t1024_kernel(tc, q_words, q_scales, k_words,
         nc.vector.tensor_copy(by_place(kb_g[:].bitcast(U32)), kb_pool[:].bitcast(U32).indirect(offsets[:]))
         ks_g = sb.tile([P, N], U8, align_bytes=64)
         nc.vector.tensor_copy(ks_g[:], ks_pool[:].indirect(offsets[:]))
-        vs_g = sb.tile([P, N], F32)
-        nc.vector.tensor_copy(by_place(vs_g[:].bitcast(U32)), vs_pool[:].bitcast(U32).indirect(offsets[:]))
         ks_p = sb.tile([P, N], U8, align_bytes=64)
         nc.vector.tensor_copy(
             ks_p[:].bitcast(I32).rearrange("p (t g w) -> p t g w", t=PACK, w=RUN // 4),
@@ -76,10 +74,12 @@ def tile_attend_silu_kb_topkq256n512t1024_kernel(tc, q_words, q_scales, k_words,
         kw_g = sb.tile([P, N], U32, align_bytes=64)
         nc.vector.tensor_copy(by_place(kw_g[:]), kw_pool[:].bitcast(U32).indirect(offsets[:]))
 
-        v_bf = sb.tile([P, T], BF16)
-        nc.scalar.activation(v_bf[:], v_pool[:], ACT.Copy)
+        vs_g = sb.tile([P, N], F32)
+        nc.vector.tensor_copy(by_place(vs_g[:].bitcast(U32)), vs_pool[:].bitcast(U32).indirect(offsets[:]))
         v_g = sb.tile([P, N], BF16)
-        nc.scalar.activation(v_g[:].rearrange("p (g r t) -> p g t r", t=PACK, r=RUN), v_bf[:].indirect(offsets[:]), ACT.Copy)
+        nc.vector.tensor_copy(
+            v_g[:].rearrange("p (u g r e) -> p g u e r", u=2, r=RUN, e=2), v_pool[:].indirect(offsets[:])
+        )
 
         kb_t = ps.tile([P, PACK, P], F32, tag="bank4")
         for t in range(PACK):
@@ -87,43 +87,38 @@ def tile_attend_silu_kb_topkq256n512t1024_kernel(tc, q_words, q_scales, k_words,
         kb_col = sb.tile([P, PACK], F32)
         nc.scalar.copy(kb_col[:], kb_t[:, :, LIVE])
 
-        vs_t = ps.tile([P, PACK, P], F32, tag="bank7")
-        for t in range(PACK):
-            nc.tensor.transpose(vs_t[:, t, :], vs_g[:, t * P : (t + 1) * P], ident32[:])
-
-        v_t = ps.tile([P, 2, P], F32, tag="bank5")
-        v_pairs = v_g[:].bitcast(F32)
-        for u in range(2):
-            nc.tensor.transpose(v_t[:, u, :], v_pairs[:, u : 2 * P : 2], ident32[:])
-        v_in = sb.tile([P, DV * PACK], BF16, align_bytes=64)
-        nc.scalar.copy(v_in[:].bitcast(F32).rearrange("p (e u) -> p e u", u=2), v_t[:].rearrange("p u e -> p e u"))
-        v_codes = sb.tile([P, DV], U32, align_bytes=64)
-        v_scales = sb.tile([P, DV], U8, align_bytes=64)
-        nc.vector.quantize_mx(out=v_codes[:].bitcast(FP8X4), scales=v_scales[:], in_=v_in[:])
-
         halves = NQ // P
-        vs_col = vs_t[:, :, LIVE : LIVE + 1].unsqueeze(1).to_broadcast([P, P // 2, PACK, 2])
         p_t = sb.tile([P, PACK, NQ], F32)
-
-        def weigh(t, queries, bank):
-            score = ps.tile([P, queries.stop - queries.start], F32, name="score", tag="bank%d" % bank)
-            cols = slice(t * P, (t + 1) * P)
-            nc.tensor.matmul_mx(
-                out=score[:],
-                lhsT=kw_g[:, cols].bitcast(FP8X4),
-                lhsT_scale=ks_p[:, cols],
-                rhs=qw[:, queries].bitcast(FP8X4),
-                rhs_scale=qs[:, queries],
-                start=True,
-                stop=True,
-            )
-            nc.scalar.activation(p_t[:, t, queries], score[:], ACT.Silu, bias=kb_col[:, t : t + 1])
-
-        w_in = []
         for h in range(halves):
             queries = slice(h * P, (h + 1) * P)
             for t in range(PACK):
-                weigh(t, queries, (PACK * h + t) % 7)
+                score = ps.tile([P, P], F32, name="score", tag="bank%d" % (PACK * h + t))
+                cols = slice(t * P, (t + 1) * P)
+                nc.tensor.matmul_mx(
+                    out=score[:],
+                    lhsT=kw_g[:, cols].bitcast(FP8X4),
+                    lhsT_scale=ks_p[:, cols],
+                    rhs=qw[:, queries].bitcast(FP8X4),
+                    rhs_scale=qs[:, queries],
+                    start=True,
+                    stop=True,
+                )
+                nc.scalar.activation(p_t[:, t, queries], score[:], ACT.Silu, bias=kb_col[:, t : t + 1])
+
+        vs_t = ps.tile([P, PACK, P], F32, tag="bank0")
+        for t in range(PACK):
+            nc.tensor.transpose(vs_t[:, t, :], vs_g[:, t * P : (t + 1) * P], ident32[:])
+        v_t = ps.tile([P, 2, P], F32, tag="bank1")
+        v_pairs = v_g[:].bitcast(F32)
+        for u in range(2):
+            nc.tensor.transpose(v_t[:, u, :], v_pairs[:, u * P : (u + 1) * P], ident32[:])
+        v_in = sb.tile([P, DV * PACK], BF16, align_bytes=64)
+        nc.scalar.copy(v_in[:].bitcast(F32).rearrange("p (e u) -> p e u", u=2), v_t[:].rearrange("p u e -> p e u"))
+
+        vs_col = vs_t[:, :, LIVE : LIVE + 1].unsqueeze(1).to_broadcast([P, P // 2, PACK, 2])
+        w_in = []
+        for h in range(halves):
+            queries = slice(h * P, (h + 1) * P)
             w_h = sb.tile([P, P, PACK], BF16, name="w_in%d" % h, align_bytes=64)
             nc.vector.tensor_tensor(
                 w_h[:].rearrange("p (c i) t -> p c t i", i=2),
@@ -133,11 +128,15 @@ def tile_attend_silu_kb_topkq256n512t1024_kernel(tc, q_words, q_scales, k_words,
             )
             w_in.append(w_h)
 
+        v_codes = sb.tile([P, DV], U32, align_bytes=64)
+        v_scales = sb.tile([P, DV], U8, align_bytes=64)
+        nc.vector.quantize_mx(out=v_codes[:].bitcast(FP8X4), scales=v_scales[:], in_=v_in[:])
+
         for h in range(halves):
             w_codes = sb.tile([P, P], U32, name="w_codes%d" % h, align_bytes=64)
             w_scales = sb.tile([P, P], U8, name="w_scales%d" % h, align_bytes=64)
             nc.vector.quantize_mx(out=w_codes[:].bitcast(FP8X4), scales=w_scales[:], in_=w_in[h][:].rearrange("p q t -> p (q t)"))
-            y = ps.tile([P, DV], F32, name="y%d" % h, tag="bank%d" % (h + 1))
+            y = ps.tile([P, DV], F32, name="y%d" % h, tag="bank%d" % (h + 2))
             nc.tensor.matmul_mx(
                 out=y[:],
                 lhsT=w_codes[:].bitcast(FP8X4),

@@ -89,21 +89,19 @@ def tile_attend_silu_kb_topkq256n512t1024_kernel(tc, q_words, q_scales, k_words,
 
         halves = NQ // P
         p_t = sb.tile([P, PACK, NQ], F32)
-        for h in range(halves):
-            queries = slice(h * P, (h + 1) * P)
-            for t in range(PACK):
-                score = ps.tile([P, P], F32, name="score", tag="bank%d" % (PACK * h + t))
-                cols = slice(t * P, (t + 1) * P)
-                nc.tensor.matmul_mx(
-                    out=score[:],
-                    lhsT=kw_g[:, cols].bitcast(FP8X4),
-                    lhsT_scale=ks_p[:, cols],
-                    rhs=qw[:, queries].bitcast(FP8X4),
-                    rhs_scale=qs[:, queries],
-                    start=True,
-                    stop=True,
-                )
-                nc.scalar.activation(p_t[:, t, queries], score[:], ACT.Silu, bias=kb_col[:, t : t + 1])
+        for t in range(PACK):
+            score = ps.tile([P, NQ], F32, name="score", tag="bank%d" % t)
+            cols = slice(t * P, (t + 1) * P)
+            nc.tensor.matmul_mx(
+                out=score[:],
+                lhsT=kw_g[:, cols].bitcast(FP8X4),
+                lhsT_scale=ks_p[:, cols],
+                rhs=qw[:].bitcast(FP8X4),
+                rhs_scale=qs[:],
+                start=True,
+                stop=True,
+            )
+            nc.scalar.activation(p_t[:, t, :], score[:], ACT.Silu, bias=kb_col[:, t : t + 1])
 
         vs_t = ps.tile([P, PACK, P], F32, tag="bank0")
         for t in range(PACK):

@@ -29,6 +29,7 @@ def tile_attend_silu_kb_topkq256n512t1024_kernel(tc, q_words, q_scales, k_words,
     nc = tc.nc
     with ExitStack() as ctx:
         sb = ctx.enter_context(tc.tile_pool(name="sb", bufs=1))
+        shared = ctx.enter_context(tc.tile_pool(name="shared", bufs=1))
         ps = ctx.enter_context(tc.psum_pool(name="ps", bufs=1))
 
         offsets = sb.tile([P, N // 16], U16)
@@ -62,28 +63,28 @@ def tile_attend_silu_kb_topkq256n512t1024_kernel(tc, q_words, q_scales, k_words,
         for Q in range(4):
             nc.sync.dma_start(qs[32 * Q : 32 * Q + 4, :].bitcast(I32), q_scales[0, 0, 4 * Q : 4 * Q + 4, :].bitcast(I32))
 
-        kb_g = sb.tile([P, N], F32)
+        kb_g = shared.tile([P, N], F32, offset=512, align_bytes=64)
         nc.vector.tensor_copy(by_place(kb_g[:].bitcast(U32)), kb_pool[:].bitcast(U32).indirect(offsets[:]))
         ks_g = sb.tile([P, N], U8, align_bytes=64)
         nc.vector.tensor_copy(ks_g[:], ks_pool[:].indirect(offsets[:]))
-        ks_p = sb.tile([P, N], U8, align_bytes=64)
-        nc.vector.tensor_copy(
-            ks_p[:].bitcast(I32).rearrange("p (t g w) -> p t g w", t=PACK, w=RUN // 4),
-            ks_g[:].bitcast(I32).rearrange("p (g t w) -> p t g w", t=PACK, w=RUN // 4),
-        )
         kw_g = sb.tile([P, N], U32, align_bytes=64)
         nc.vector.tensor_copy(by_place(kw_g[:]), kw_pool[:].bitcast(U32).indirect(offsets[:]))
-
-        vs_g = sb.tile([P, N], F32)
-        nc.vector.tensor_copy(by_place(vs_g[:].bitcast(U32)), vs_pool[:].bitcast(U32).indirect(offsets[:]))
-        v_g = sb.tile([P, N], BF16)
-        nc.vector.tensor_copy(
-            v_g[:].rearrange("p (u g r e) -> p g u e r", u=2, r=RUN, e=2), v_pool[:].indirect(offsets[:])
-        )
 
         kb_t = ps.tile([P, PACK, P], F32, tag="bank4")
         for t in range(PACK):
             nc.tensor.transpose(kb_t[:, t, :], kb_g[:, t * P : (t + 1) * P], ident32[:])
+        ks_p = shared.tile([P, N], U8, offset=1024, align_bytes=64)
+        nc.vector.tensor_copy(
+            ks_p[:].bitcast(I32).rearrange("p (t g w) -> p t g w", t=PACK, w=RUN // 4),
+            ks_g[:].bitcast(I32).rearrange("p (g t w) -> p t g w", t=PACK, w=RUN // 4),
+        )
+        vs_g = shared.tile([P, N], F32, offset=1536, align_bytes=64)
+        nc.vector.tensor_copy(by_place(vs_g[:].bitcast(U32)), vs_pool[:].bitcast(U32).indirect(offsets[:]))
+        v_g = shared.tile([P, N], BF16, offset=0, align_bytes=64)
+        nc.vector.tensor_copy(
+            v_g[:].rearrange("p (u g r e) -> p g u e r", u=2, r=RUN, e=2), v_pool[:].indirect(offsets[:])
+        )
+
         kb_col = sb.tile([P, PACK], F32)
         nc.scalar.copy(kb_col[:], kb_t[:, :, LIVE])
 

@@ -90,19 +90,21 @@ def tile_attend_silu_kb_topkq256n512t1024_kernel(tc, q_words, q_scales, k_words,
 
         halves = NQ // P
         p_t = sb.tile([P, PACK, NQ], F32)
-        for t in range(PACK):
-            score = ps.tile([P, NQ], F32, name="score", tag="bank%d" % t)
-            cols = slice(t * P, (t + 1) * P)
-            nc.tensor.matmul_mx(
-                out=score[:],
-                lhsT=kw_g[:, cols].bitcast(FP8X4),
-                lhsT_scale=ks_p[:, cols],
-                rhs=qw[:].bitcast(FP8X4),
-                rhs_scale=qs[:],
-                start=True,
-                stop=True,
-            )
-            nc.scalar.activation(p_t[:, t, :], score[:], ACT.Silu, bias=kb_col[:, t : t + 1])
+        for h in range(halves):
+            queries = slice(h * P, (h + 1) * P)
+            for t in range(PACK):
+                score = ps.tile([P, P], F32, name="score", tag="bank%d" % (PACK * h + t))
+                cols = slice(t * P, (t + 1) * P)
+                nc.tensor.matmul_mx(
+                    out=score[:],
+                    lhsT=kw_g[:, cols].bitcast(FP8X4),
+                    lhsT_scale=ks_p[:, cols],
+                    rhs=qw[:, queries].bitcast(FP8X4),
+                    rhs_scale=qs[:, queries],
+                    start=True,
+                    stop=True,
+                )
+                nc.scalar.activation(p_t[:, t, queries], score[:], ACT.Silu, bias=kb_col[:, t : t + 1])
 
         vs_t = ps.tile([P, PACK, P], F32, tag="bank0")
         for t in range(PACK):
@@ -127,14 +129,14 @@ def tile_attend_silu_kb_topkq256n512t1024_kernel(tc, q_words, q_scales, k_words,
             )
             w_in.append(w_h)
 
-        v_codes = sb.tile([P, DV], U32, align_bytes=64)
-        v_scales = sb.tile([P, DV], U8, align_bytes=64)
-        nc.vector.quantize_mx(out=v_codes[:].bitcast(FP8X4), scales=v_scales[:], in_=v_in[:])
-
         for h in range(halves):
             w_codes = sb.tile([P, P], U32, name="w_codes%d" % h, align_bytes=64)
             w_scales = sb.tile([P, P], U8, name="w_scales%d" % h, align_bytes=64)
             nc.vector.quantize_mx(out=w_codes[:].bitcast(FP8X4), scales=w_scales[:], in_=w_in[h][:].rearrange("p q t -> p (q t)"))
+            if h == 0:
+                v_codes = sb.tile([P, DV], U32, align_bytes=64)
+                v_scales = sb.tile([P, DV], U8, align_bytes=64)
+                nc.vector.quantize_mx(out=v_codes[:].bitcast(FP8X4), scales=v_scales[:], in_=v_in[:])
             y = ps.tile([P, DV], F32, name="y%d" % h, tag="bank%d" % (h + 2))
             nc.tensor.matmul_mx(
                 out=y[:],

@@ -129,6 +129,7 @@ def tile_attend_silu_kb_topkq256n512t1024_kernel(tc, q_words, q_scales, k_words,
             )
             w_in.append(w_h)
 
+        res = sb.tile([P, halves, DV], F32)
         for h in range(halves):
             w_codes = sb.tile([P, P], U32, name="w_codes%d" % h, align_bytes=64)
             w_scales = sb.tile([P, P], U8, name="w_scales%d" % h, align_bytes=64)
@@ -147,10 +148,8 @@ def tile_attend_silu_kb_topkq256n512t1024_kernel(tc, q_words, q_scales, k_words,
                 start=True,
                 stop=True,
             )
-            res = sb.tile([P, DV], F32, name="res%d" % h)
             if h == 0:
-                nc.scalar.activation(res[:], y[:], ACT.Copy, scale=1.0 / 16.0)
-                nc.scalar.dma_start(out[0, h * P : (h + 1) * P, :], res[:])
+                nc.scalar.activation(res[:, h, :], y[:], ACT.Copy, scale=1.0 / 16.0)
             else:
-                nc.vector.tensor_scalar(res[:], y[:], 1.0 / 16.0, None, ALU.mult)
-                nc.sync.dma_start(out[0, h * P : (h + 1) * P, :], res[:])
+                nc.vector.tensor_scalar(res[:, h, :], y[:], 1.0 / 16.0, None, ALU.mult)
+        nc.sync.dma_start(out[0].rearrange("(h p) e -> p h e", p=P), res[:])

@@ -49,8 +49,8 @@ def tile_attend_silu_kb_topkq256n512t1024_kernel(tc, q_words, q_scales, k_words,
         ident32 = sb.tile([P, P], F32)
         make_identity(nc, ident32[:])
 
-        nc.scalar.dma_start(kb_pool[LIVE:P, :], kb[LIVE:P, :])
         nc.sync.dma_start(offsets[:], offs)
+        nc.sync.dma_start(kb_pool[LIVE:P, :], kb[LIVE:P, :])
         for Q in range(4):
             rows = k_scales[0, 4 * Q : 4 * Q + 4, :].bitcast(I32).unsqueeze(0).to_broadcast([8, 4, T // 4])
             nc.sync.dma_start(ks_pool[32 * Q : 32 * Q + 32, :].bitcast(I32), rows)

@@ -57,11 +57,11 @@ def tile_attend_silu_kb_topkq256n512t1024_kernel(tc, q_words, q_scales, k_words,
         nc.sync.dma_start(kw_pool[:], k_words[0].rearrange("p n r -> p (n r)").bitcast(I32))
         nc.sync.dma_start(qw[:], q_words[0, 0].rearrange("p n r -> p (n r)").bitcast(I32))
         nc.sync.dma_start(vs_pool[LIVE:P, :], vs[LIVE:P, :])
-        nc.sync.dma_start(v_pool[:], vT)
         warm_out = sb.tile([P, 8], F32)
         nc.scalar.activation(warm_out[:], warm[:], ACT.Silu)
         for Q in range(4):
             nc.sync.dma_start(qs[32 * Q : 32 * Q + 4, :].bitcast(I32), q_scales[0, 0, 4 * Q : 4 * Q + 4, :].bitcast(I32))
+        nc.sync.dma_start(v_pool[:], vT)
 
         kb_g = shared.tile([P, N], F32, offset=512, align_bytes=64)
         nc.vector.tensor_copy(by_place(kb_g[:].bitcast(U32)), kb_pool[:].bitcast(U32).indirect(offsets[:]))
@@ -152,4 +152,4 @@ def tile_attend_silu_kb_topkq256n512t1024_kernel(tc, q_words, q_scales, k_words,
                 nc.scalar.activation(res[:, h, :], y[:], ACT.Copy, scale=1.0 / 16.0)
             else:
                 nc.vector.tensor_scalar(res[:, h, :], y[:], 1.0 / 16.0, None, ALU.mult)
-        nc.sync.dma_start(out[0].rearrange("(h p) e -> p h e", p=P), res[:])
+            nc.sync.dma_start(out[0, h * P : (h + 1) * P, :], res[:, h, :])

@@ -41,6 +41,7 @@ def tile_attend_silu_kb_topkq256n512t1024_kernel(tc, q_words, q_scales, k_words,
         qw = sb.tile([P, NQ], I32, align_bytes=64)
         qs = sb.tile([P, NQ], U8, align_bytes=64)
 
+        nc.gpsimd.memset(ks_pool[:].bitcast(I32), 0)
         warm = sb.tile([P, 8], F32)
         nc.vector.memset(warm[:], 0.0)
         nc.vector.memset(kb_pool[0:LIVE, :], 0.0)
@@ -52,8 +53,7 @@ def tile_attend_silu_kb_topkq256n512t1024_kernel(tc, q_words, q_scales, k_words,
         nc.sync.dma_start(offsets[:], offs)
         nc.sync.dma_start(kb_pool[LIVE:P, :], kb[LIVE:P, :])
         for Q in range(4):
-            rows = k_scales[0, 4 * Q : 4 * Q + 4, :].bitcast(I32).unsqueeze(0).to_broadcast([8, 4, T // 4])
-            nc.sync.dma_start(ks_pool[32 * Q : 32 * Q + 32, :].bitcast(I32), rows)
+            nc.sync.dma_start(ks_pool[32 * Q : 32 * Q + 4, :].bitcast(I32), k_scales[0, 4 * Q : 4 * Q + 4, :].bitcast(I32))
         nc.sync.dma_start(kw_pool[:], k_words[0].rearrange("p n r -> p (n r)").bitcast(I32))
         nc.sync.dma_start(qw[:], q_words[0, 0].rearrange("p n r -> p (n r)").bitcast(I32))
         nc.sync.dma_start(vs_pool[LIVE:P, :], vs[LIVE:P, :])

@@ -41,14 +41,15 @@ def tile_attend_silu_kb_topkq256n512t1024_kernel(tc, q_words, q_scales, k_words,
         qw = sb.tile([P, NQ], I32, align_bytes=64)
         qs = sb.tile([P, NQ], U8, align_bytes=64)
 
-        nc.gpsimd.memset(ks_pool[:].bitcast(I32), 0)
+        nc.vector.memset(ks_pool[:].bitcast(I32), 0)
+        ident32 = sb.tile([P, P], F32)
+        nc.vector.memset(ident32[:], 0.0)
+        make_identity(nc, ident32[:], nomemset=True)
         warm = sb.tile([P, 8], F32)
         nc.vector.memset(warm[:], 0.0)
         nc.vector.memset(kb_pool[0:LIVE, :], 0.0)
-        nc.vector.memset(vs_pool[0:LIVE, :], 0.0)
         nc.vector.memset(qs[:].bitcast(I32), 0)
-        ident32 = sb.tile([P, P], F32)
-        make_identity(nc, ident32[:])
+        nc.vector.memset(vs_pool[0:LIVE, :], 0.0)
 
         nc.sync.dma_start(offsets[:], offs)
         nc.sync.dma_start(kb_pool[LIVE:P, :], kb[LIVE:P, :])

@@ -17,6 +17,7 @@ P = 128
 PACK = 4
 RUN = 8
 LIVE = 127
+SHARE = 32
 T, N, NQ, D, DV = 1024, 512, 256, 512, 128
 FLOPS = 2 * D * N * NQ + 2 * N * NQ * DV
 
@@ -117,18 +118,25 @@ def tile_attend_silu_kb_topkq256n512t1024_kernel(tc, q_words, q_scales, k_words,
         v_in = sb.tile([P, DV * PACK], BF16, align_bytes=64)
         nc.scalar.copy(v_in[:].bitcast(F32).rearrange("p (e u) -> p e u", u=2), v_t[:].rearrange("p u e -> p e u"))
 
-        vs_col = vs_t[:, :, LIVE : LIVE + 1].unsqueeze(1).to_broadcast([P, P // 2, PACK, 2])
+        vs_sb = sb.tile([P, PACK], F32)
+        nc.vector.tensor_copy(vs_sb[:], vs_t[:, :, LIVE])
         w_in = []
         for h in range(halves):
-            queries = slice(h * P, (h + 1) * P)
+            n = P if h == 0 else P - SHARE
             w_h = sb.tile([P, P, PACK], BF16, name="w_in%d" % h, align_bytes=64)
             nc.vector.tensor_tensor(
-                w_h[:].rearrange("p (c i) t -> p c t i", i=2),
-                p_t[:, :, queries].rearrange("p t (c i) -> p c t i", i=2),
-                vs_col,
+                w_h[:, :n, :].rearrange("p (c i) t -> p c t i", i=2),
+                p_t[:, :, h * P : h * P + n].rearrange("p t (c i) -> p c t i", i=2),
+                vs_t[:, :, LIVE : LIVE + 1].unsqueeze(1).to_broadcast([P, n // 2, PACK, 2]),
                 ALU.mult,
             )
             w_in.append(w_h)
+        nc.gpsimd.tensor_tensor(
+            w_in[1][:, P - SHARE :, :].rearrange("p (c i) t -> p c t i", i=2),
+            p_t[:, :, NQ - SHARE :].rearrange("p t (c i) -> p c t i", i=2),
+            vs_sb[:].unsqueeze(2).unsqueeze(1).to_broadcast([P, SHARE // 2, PACK, 2]),
+            ALU.mult,
+        )
 
         res = sb.tile([P, halves, DV], F32)
         for h in range(halves):

@@ -44,13 +44,14 @@ def tile_attend_silu_kb_topkq256n512t1024_kernel(tc, q_words, q_scales, k_words,
 
         nc.vector.memset(ks_pool[:].bitcast(I32), 0)
         ident32 = sb.tile([P, P], F32)
+        nc.vector.memset(qs[:].bitcast(I32), 0)
+        nc.vector.memset(kb_pool[0:LIVE, :], 0.0)
         nc.vector.memset(ident32[:], 0.0)
         make_identity(nc, ident32[:], nomemset=True)
-        warm = sb.tile([P, 8], F32)
-        nc.vector.memset(warm[:], 0.0)
-        nc.vector.memset(kb_pool[0:LIVE, :], 0.0)
-        nc.vector.memset(qs[:].bitcast(I32), 0)
-        nc.vector.memset(vs_pool[0:LIVE, :], 0.0)
+        nc.vector.memset(vs_pool[0:LIVE, 0:8], 0.0)
+        warm_out = sb.tile([P, 8], F32)
+        nc.scalar.activation(warm_out[0:LIVE, :], vs_pool[0:LIVE, 0:8], ACT.Silu)
+        nc.gpsimd.memset(vs_pool[0:LIVE, :], 0.0)
 
         nc.sync.dma_start(offsets[:], offs)
         nc.sync.dma_start(kb_pool[LIVE:P, :], kb[LIVE:P, :])
@@ -59,8 +60,6 @@ def tile_attend_silu_kb_topkq256n512t1024_kernel(tc, q_words, q_scales, k_words,
         nc.sync.dma_start(kw_pool[:], k_words[0].rearrange("p n r -> p (n r)").bitcast(I32))
         nc.sync.dma_start(qw[:], q_words[0, 0].rearrange("p n r -> p (n r)").bitcast(I32))
         nc.sync.dma_start(vs_pool[LIVE:P, :], vs[LIVE:P, :])
-        warm_out = sb.tile([P, 8], F32)
-        nc.scalar.activation(warm_out[:], warm[:], ACT.Silu)
         for Q in range(4):
             nc.sync.dma_start(qs[32 * Q : 32 * Q + 4, :].bitcast(I32), q_scales[0, 0, 4 * Q : 4 * Q + 4, :].bitcast(I32))
         nc.sync.dma_start(v_pool[:], vT)

@@ -17,6 +17,7 @@ P = 128
 PACK = 4
 RUN = 8
 LIVE = 127
+PAIR = 126
 SHARE = 32
 T, N, NQ, D, DV = 1024, 512, 256, 512, 128
 FLOPS = 2 * D * N * NQ + 2 * N * NQ * DV
@@ -48,20 +49,20 @@ def tile_attend_silu_kb_topkq256n512t1024_kernel(tc, q_words, q_scales, k_words,
         nc.vector.memset(kb_pool[0:LIVE, :], 0.0)
         nc.vector.memset(ident32[:], 0.0)
         make_identity(nc, ident32[:], nomemset=True)
-        nc.vector.memset(vs_pool[0:LIVE, 0:8], 0.0)
+        nc.vector.memset(vs_pool[0:PAIR, 0:8], 0.0)
         warm_out = sb.tile([P, 8], F32)
-        nc.scalar.activation(warm_out[0:LIVE, :], vs_pool[0:LIVE, 0:8], ACT.Silu)
-        nc.gpsimd.memset(vs_pool[0:LIVE, :], 0.0)
+        nc.scalar.activation(warm_out[0:PAIR, :], vs_pool[0:PAIR, 0:8], ACT.Silu)
+        nc.gpsimd.memset(vs_pool[0:PAIR, :], 0.0)
 
         nc.sync.dma_start(offsets[:], offs)
         nc.sync.dma_start(kb_pool[LIVE:P, :], kb[LIVE:P, :])
-        for Q in range(4):
-            nc.sync.dma_start(ks_pool[32 * Q : 32 * Q + 4, :].bitcast(I32), k_scales[0, 4 * Q : 4 * Q + 4, :].bitcast(I32))
+        for f in range(4):
+            nc.sync.dma_start(ks_pool[f:P:32, :].bitcast(I32), k_scales[0, f:16:4, :].bitcast(I32))
         nc.sync.dma_start(kw_pool[:], k_words[0].rearrange("p n r -> p (n r)").bitcast(I32))
         nc.sync.dma_start(qw[:], q_words[0, 0].rearrange("p n r -> p (n r)").bitcast(I32))
-        nc.sync.dma_start(vs_pool[LIVE:P, :], vs[LIVE:P, :])
-        for Q in range(4):
-            nc.sync.dma_start(qs[32 * Q : 32 * Q + 4, :].bitcast(I32), q_scales[0, 0, 4 * Q : 4 * Q + 4, :].bitcast(I32))
+        nc.sync.dma_start(vs_pool[PAIR:P, :], vs[PAIR:P, :])
+        for f in range(4):
+            nc.sync.dma_start(qs[f:P:32, :].bitcast(I32), q_scales[0, 0, f:16:4, :].bitcast(I32))
         nc.sync.dma_start(v_pool[:], vT)
 
         kb_g = shared.tile([P, N], F32, offset=512, align_bytes=64)
@@ -126,7 +127,7 @@ def tile_attend_silu_kb_topkq256n512t1024_kernel(tc, q_words, q_scales, k_words,
             nc.vector.tensor_tensor(
                 w_h[:, :n, :].rearrange("p (c i) t -> p c t i", i=2),
                 p_t[:, :, h * P : h * P + n].rearrange("p t (c i) -> p c t i", i=2),
-                vs_t[:, :, LIVE : LIVE + 1].unsqueeze(1).to_broadcast([P, n // 2, PACK, 2]),
+                vs_t[:, :, PAIR:P].unsqueeze(1).to_broadcast([P, n // 2, PACK, 2]),
                 ALU.mult,
             )
             w_in.append(w_h)

@@ -115,8 +115,14 @@ def tile_attend_silu_kb_topkq256n512t1024_kernel(tc, q_words, q_scales, k_words,
         v_pairs = v_g[:].bitcast(F32)
         for u in range(2):
             nc.tensor.transpose(v_t[:, u, :], v_pairs[:, u * P : (u + 1) * P], ident32[:])
-        v_in = sb.tile([P, DV * PACK], BF16, align_bytes=64)
-        nc.scalar.copy(v_in[:].bitcast(F32).rearrange("p (e u) -> p e u", u=2), v_t[:].rearrange("p u e -> p e u"))
+        v_in = []
+        for c in range(2):
+            v_c = sb.tile([P, DV // 2 * PACK], BF16, name="v_in%d" % c, align_bytes=64)
+            features = slice(c * DV // 2, (c + 1) * DV // 2)
+            nc.scalar.copy(
+                v_c[:].bitcast(F32).rearrange("p (e u) -> p e u", u=2), v_t[:, :, features].rearrange("p u e -> p e u")
+            )
+            v_in.append(v_c)
 
         vs_sb = sb.tile([P, PACK], F32)
         nc.vector.tensor_copy(vs_sb[:], vs_t[:, :, LIVE])
@@ -138,15 +144,20 @@ def tile_attend_silu_kb_topkq256n512t1024_kernel(tc, q_words, q_scales, k_words,
             ALU.mult,
         )
 
-        res = sb.tile([P, halves, DV], F32)
+        w_mx = []
         for h in range(halves):
             w_codes = sb.tile([P, P], U32, name="w_codes%d" % h, align_bytes=64)
             w_scales = sb.tile([P, P], U8, name="w_scales%d" % h, align_bytes=64)
             nc.vector.quantize_mx(out=w_codes[:].bitcast(FP8X4), scales=w_scales[:], in_=w_in[h][:].rearrange("p q t -> p (q t)"))
-            if h == 0:
-                v_codes = sb.tile([P, DV], U32, align_bytes=64)
-                v_scales = sb.tile([P, DV], U8, align_bytes=64)
-                nc.vector.quantize_mx(out=v_codes[:].bitcast(FP8X4), scales=v_scales[:], in_=v_in[:])
+            w_mx.append((w_codes, w_scales))
+        v_codes = sb.tile([P, DV], U32, align_bytes=64)
+        v_scales = sb.tile([P, DV], U8, align_bytes=64)
+        for c in range(2):
+            features = slice(c * DV // 2, (c + 1) * DV // 2)
+            nc.vector.quantize_mx(out=v_codes[:, features].bitcast(FP8X4), scales=v_scales[:, features], in_=v_in[c][:])
+
+        res = sb.tile([P, halves, DV], F32)
+        for h, (w_codes, w_scales) in enumerate(w_mx):
             y = ps.tile([P, DV], F32, name="y%d" % h, tag="bank%d" % (h + 2))
             nc.tensor.matmul_mx(
                 out=y[:],

@@ -15,23 +15,19 @@ ALU = mybir.AluOpType
 
 P = 128
 PACK = 4
-RUN = 8
 LIVE = 127
-PAIR = 126
-SHARE = 32
 T, N, NQ, D, DV = 1024, 512, 256, 512, 128
 FLOPS = 2 * D * N * NQ + 2 * N * NQ * DV
 
 
 def by_place(tile):
-    return tile.rearrange("p (t g r) -> p g t r", t=PACK, r=RUN)
+    return tile.rearrange("p (t s) -> p s t", t=PACK)
 
 
 def tile_attend_silu_kb_topkq256n512t1024_kernel(tc, q_words, q_scales, k_words, k_scales, vT, vs, kb, offs, out):
     nc = tc.nc
     with ExitStack() as ctx:
         sb = ctx.enter_context(tc.tile_pool(name="sb", bufs=1))
-        shared = ctx.enter_context(tc.tile_pool(name="shared", bufs=1))
         ps = ctx.enter_context(tc.psum_pool(name="ps", bufs=1))
 
         offsets = sb.tile([P, N // 16], U16)
@@ -42,53 +38,48 @@ def tile_attend_silu_kb_topkq256n512t1024_kernel(tc, q_words, q_scales, k_words,
         v_pool = sb.tile([P, T], F32)
         qw = sb.tile([P, NQ], I32, align_bytes=64)
         qs = sb.tile([P, NQ], U8, align_bytes=64)
+        ident32 = sb.tile([P, P], F32)
 
         nc.vector.memset(ks_pool[:].bitcast(I32), 0)
-        ident32 = sb.tile([P, P], F32)
-        nc.vector.memset(qs[:].bitcast(I32), 0)
+        warm_in = sb.tile([P, 8], F32)
+        nc.vector.memset(warm_in[:], 0.0)
+        warm_out = sb.tile([P, 8], F32)
+        nc.scalar.activation(warm_out[:], warm_in[:], ACT.Silu)
         nc.vector.memset(kb_pool[0:LIVE, :], 0.0)
+        nc.vector.memset(qs[:].bitcast(I32), 0)
         nc.vector.memset(ident32[:], 0.0)
         make_identity(nc, ident32[:], nomemset=True)
-        nc.vector.memset(vs_pool[0:PAIR, 0:8], 0.0)
-        warm_out = sb.tile([P, 8], F32)
-        nc.scalar.activation(warm_out[0:PAIR, :], vs_pool[0:PAIR, 0:8], ACT.Silu)
-        nc.gpsimd.memset(vs_pool[0:PAIR, :], 0.0)
+        nc.vector.memset(vs_pool[0:LIVE, :], 0.0)
 
         nc.sync.dma_start(offsets[:], offs)
         nc.sync.dma_start(kb_pool[LIVE:P, :], kb[LIVE:P, :])
         for f in range(4):
             nc.sync.dma_start(ks_pool[f:P:32, :].bitcast(I32), k_scales[0, f:16:4, :].bitcast(I32))
+        nc.sync.dma_start(vs_pool[LIVE:P, :], vs[LIVE:P, :])
         nc.sync.dma_start(kw_pool[:], k_words[0].rearrange("p n r -> p (n r)").bitcast(I32))
         nc.sync.dma_start(qw[:], q_words[0, 0].rearrange("p n r -> p (n r)").bitcast(I32))
-        nc.sync.dma_start(vs_pool[PAIR:P, :], vs[PAIR:P, :])
         for f in range(4):
             nc.sync.dma_start(qs[f:P:32, :].bitcast(I32), q_scales[0, 0, f:16:4, :].bitcast(I32))
         nc.sync.dma_start(v_pool[:], vT)
 
-        kb_g = shared.tile([P, N], F32, offset=512, align_bytes=64)
-        nc.vector.tensor_copy(by_place(kb_g[:].bitcast(U32)), kb_pool[:].bitcast(U32).indirect(offsets[:]))
+        kb_g = sb.tile([P, N], F32)
+        nc.scalar.activation(kb_g[:], kb_pool[:].indirect(offsets[:]), ACT.Copy)
+        vs_g = sb.tile([P, N], F32)
+        nc.scalar.activation(vs_g[:], vs_pool[:].indirect(offsets[:]), ACT.Copy)
+        kb_col = sb.tile([P, PACK], F32)
+        kb_t = ps.tile([P, PACK, P], F32, tag="bank7")
+        for t in range(PACK):
+            nc.tensor.transpose(kb_t[:, t, :], kb_g[:, t:N:PACK], ident32[:])
+        nc.scalar.copy(kb_col[:], kb_t[:, :, LIVE])
+        vs_col = sb.tile([P, PACK], F32)
+        nc.sync.dma_start(vs_col[:], vs_g[LIVE:P, :].rearrange("o (p t) -> o p t", t=PACK))
+
         ks_g = sb.tile([P, N], U8, align_bytes=64)
-        nc.vector.tensor_copy(ks_g[:], ks_pool[:].indirect(offsets[:]))
+        nc.vector.tensor_copy(by_place(ks_g[:]), ks_pool[:].indirect(offsets[:]))
         kw_g = sb.tile([P, N], U32, align_bytes=64)
         nc.vector.tensor_copy(by_place(kw_g[:]), kw_pool[:].bitcast(U32).indirect(offsets[:]))
-
-        kb_t = ps.tile([P, PACK, P], F32, tag="bank4")
-        for t in range(PACK):
-            nc.tensor.transpose(kb_t[:, t, :], kb_g[:, t * P : (t + 1) * P], ident32[:])
-        ks_p = shared.tile([P, N], U8, offset=1024, align_bytes=64)
-        nc.vector.tensor_copy(
-            ks_p[:].bitcast(I32).rearrange("p (t g w) -> p t g w", t=PACK, w=RUN // 4),
-            ks_g[:].bitcast(I32).rearrange("p (g t w) -> p t g w", t=PACK, w=RUN // 4),
-        )
-        vs_g = shared.tile([P, N], F32, offset=1536, align_bytes=64)
-        nc.vector.tensor_copy(by_place(vs_g[:].bitcast(U32)), vs_pool[:].bitcast(U32).indirect(offsets[:]))
-        v_g = shared.tile([P, N], BF16, offset=0, align_bytes=64)
-        nc.vector.tensor_copy(
-            v_g[:].rearrange("p (u g r e) -> p g u e r", u=2, r=RUN, e=2), v_pool[:].indirect(offsets[:])
-        )
-
-        kb_col = sb.tile([P, PACK], F32)
-        nc.scalar.copy(kb_col[:], kb_t[:, :, LIVE])
+        v_g = sb.tile([P, N], BF16, align_bytes=64)
+        nc.vector.tensor_copy(v_g[:], v_pool[:].indirect(offsets[:]))
 
         halves = NQ // P
         p_t = sb.tile([P, PACK, NQ], F32)
@@ -100,7 +91,7 @@ def tile_attend_silu_kb_topkq256n512t1024_kernel(tc, q_words, q_scales, k_words,
                 nc.tensor.matmul_mx(
                     out=score[:],
                     lhsT=kw_g[:, cols].bitcast(FP8X4),
-                    lhsT_scale=ks_p[:, cols],
+                    lhsT_scale=ks_g[:, cols],
                     rhs=qw[:, queries].bitcast(FP8X4),
                     rhs_scale=qs[:, queries],
                     start=True,
@@ -108,57 +99,38 @@ def tile_attend_silu_kb_topkq256n512t1024_kernel(tc, q_words, q_scales, k_words,
                 )
                 nc.scalar.activation(p_t[:, t, queries], score[:], ACT.Silu, bias=kb_col[:, t : t + 1])
 
-        vs_t = ps.tile([P, PACK, P], F32, tag="bank0")
-        for t in range(PACK):
-            nc.tensor.transpose(vs_t[:, t, :], vs_g[:, t * P : (t + 1) * P], ident32[:])
-        v_t = ps.tile([P, 2, P], F32, tag="bank1")
+        v_t = ps.tile([P, 2, P], F32, tag="bank0")
         v_pairs = v_g[:].bitcast(F32)
         for u in range(2):
-            nc.tensor.transpose(v_t[:, u, :], v_pairs[:, u * P : (u + 1) * P], ident32[:])
-        v_in = []
-        for c in range(2):
-            v_c = sb.tile([P, DV // 2 * PACK], BF16, name="v_in%d" % c, align_bytes=64)
-            features = slice(c * DV // 2, (c + 1) * DV // 2)
-            nc.scalar.copy(
-                v_c[:].bitcast(F32).rearrange("p (e u) -> p e u", u=2), v_t[:, :, features].rearrange("p u e -> p e u")
-            )
-            v_in.append(v_c)
+            nc.tensor.transpose(v_t[:, u, :], v_pairs[:, u : N // 2 : 2], ident32[:])
+        v_in = sb.tile([P, DV * PACK], BF16, align_bytes=64)
+        nc.scalar.copy(v_in[:].bitcast(F32).rearrange("p (e u) -> p e u", u=2), v_t[:].rearrange("p u e -> p e u"))
 
-        vs_sb = sb.tile([P, PACK], F32)
-        nc.vector.tensor_copy(vs_sb[:], vs_t[:, :, LIVE])
         w_in = []
         for h in range(halves):
-            n = P if h == 0 else P - SHARE
             w_h = sb.tile([P, P, PACK], BF16, name="w_in%d" % h, align_bytes=64)
             nc.vector.tensor_tensor(
-                w_h[:, :n, :].rearrange("p (c i) t -> p c t i", i=2),
-                p_t[:, :, h * P : h * P + n].rearrange("p t (c i) -> p c t i", i=2),
-                vs_t[:, :, PAIR:P].unsqueeze(1).to_broadcast([P, n // 2, PACK, 2]),
+                w_h[:].rearrange("p (c i) t -> p c t i", i=2),
+                p_t[:, :, h * P : (h + 1) * P].rearrange("p t (c i) -> p c t i", i=2),
+                vs_col[:].unsqueeze(2).unsqueeze(1).to_broadcast([P, P // 2, PACK, 2]),
                 ALU.mult,
             )
             w_in.append(w_h)
-        nc.gpsimd.tensor_tensor(
-            w_in[1][:, P - SHARE :, :].rearrange("p (c i) t -> p c t i", i=2),
-            p_t[:, :, NQ - SHARE :].rearrange("p t (c i) -> p c t i", i=2),
-            vs_sb[:].unsqueeze(2).unsqueeze(1).to_broadcast([P, SHARE // 2, PACK, 2]),
-            ALU.mult,
-        )
 
+        v_codes = sb.tile([P, DV], U32, align_bytes=64)
+        v_scales = sb.tile([P, DV], U8, align_bytes=64)
         w_mx = []
         for h in range(halves):
             w_codes = sb.tile([P, P], U32, name="w_codes%d" % h, align_bytes=64)
             w_scales = sb.tile([P, P], U8, name="w_scales%d" % h, align_bytes=64)
             nc.vector.quantize_mx(out=w_codes[:].bitcast(FP8X4), scales=w_scales[:], in_=w_in[h][:].rearrange("p q t -> p (q t)"))
             w_mx.append((w_codes, w_scales))
-        v_codes = sb.tile([P, DV], U32, align_bytes=64)
-        v_scales = sb.tile([P, DV], U8, align_bytes=64)
-        for c in range(2):
-            features = slice(c * DV // 2, (c + 1) * DV // 2)
-            nc.vector.quantize_mx(out=v_codes[:, features].bitcast(FP8X4), scales=v_scales[:, features], in_=v_in[c][:])
+            if h == 0:
+                nc.vector.quantize_mx(out=v_codes[:].bitcast(FP8X4), scales=v_scales[:], in_=v_in[:])
 
         res = sb.tile([P, halves, DV], F32)
         for h, (w_codes, w_scales) in enumerate(w_mx):
-            y = ps.tile([P, DV], F32, name="y%d" % h, tag="bank%d" % (h + 2))
+            y = ps.tile([P, DV], F32, name="y%d" % h, tag="bank%d" % (h + 1))
             nc.tensor.matmul_mx(
                 out=y[:],
                 lhsT=w_codes[:].bitcast(FP8X4),

@@ -17,6 +17,9 @@ P = 128
 PACK = 4
 LIVE = 127
 T, N, NQ, D, DV = 1024, 512, 256, 512, 128
+PIECES = [(0, 64),(64, 128),(128, 192),(192, 256)]
+KB_SPLIT = 256
+V_SPLIT = 256
 FLOPS = 2 * D * N * NQ + 2 * N * NQ * DV
 
 
@@ -57,39 +60,48 @@ def tile_attend_silu_kb_topkq256n512t1024_kernel(tc, q_words, q_scales, k_words,
             nc.sync.dma_start(ks_pool[f:P:32, :].bitcast(I32), k_scales[0, f:16:4, :].bitcast(I32))
         nc.sync.dma_start(vs_pool[LIVE:P, :], vs[LIVE:P, :])
         nc.sync.dma_start(kw_pool[:], k_words[0].rearrange("p n r -> p (n r)").bitcast(I32))
+        nc.sync.dma_start(v_pool[:], vT)
         nc.sync.dma_start(qw[:], q_words[0, 0].rearrange("p n r -> p (n r)").bitcast(I32))
         for f in range(4):
             nc.sync.dma_start(qs[f:P:32, :].bitcast(I32), q_scales[0, 0, f:16:4, :].bitcast(I32))
-        nc.sync.dma_start(v_pool[:], vT)
+
+        def gather_in_two(dst, pool, split):
+            nc.vector.tensor_copy(dst[:, :split], pool[:].indirect(offsets[:, : split // 16]))
+            nc.scalar.activation(dst[:, split:], pool[:].indirect(offsets[:, split // 16 :]), ACT.Copy)
 
         kb_g = sb.tile([P, N], F32)
-        nc.scalar.activation(kb_g[:], kb_pool[:].indirect(offsets[:]), ACT.Copy)
+        gather_in_two(kb_g, kb_pool, KB_SPLIT)
         vs_g = sb.tile([P, N], F32)
         nc.scalar.activation(vs_g[:], vs_pool[:].indirect(offsets[:]), ACT.Copy)
-        kb_col = sb.tile([P, PACK], F32)
-        kb_t = ps.tile([P, PACK, P], F32, tag="bank7")
-        for t in range(PACK):
-            nc.tensor.transpose(kb_t[:, t, :], kb_g[:, t:N:PACK], ident32[:])
-        nc.scalar.copy(kb_col[:], kb_t[:, :, LIVE])
-        vs_col = sb.tile([P, PACK], F32)
-        nc.sync.dma_start(vs_col[:], vs_g[LIVE:P, :].rearrange("o (p t) -> o p t", t=PACK))
-
         ks_g = sb.tile([P, N], U8, align_bytes=64)
         nc.vector.tensor_copy(by_place(ks_g[:]), ks_pool[:].indirect(offsets[:]))
         kw_g = sb.tile([P, N], U32, align_bytes=64)
         nc.vector.tensor_copy(by_place(kw_g[:]), kw_pool[:].bitcast(U32).indirect(offsets[:]))
+
+        kb_t = ps.tile([P, PACK, P], F32, tag="bank6")
+        vs_t = ps.tile([P, PACK, P], F32, tag="bank7")
+        for turned, row in ((kb_t, kb_g), (vs_t, vs_g)):
+            for t in range(PACK):
+                nc.tensor.transpose(turned[:, t, :], row[:, t:N:PACK], ident32[:])
+        kb_col = sb.tile([P, PACK], F32)
+        nc.scalar.copy(kb_col[:], kb_t[:, :, LIVE])
+
         v_g = sb.tile([P, N], BF16, align_bytes=64)
-        nc.vector.tensor_copy(v_g[:], v_pool[:].indirect(offsets[:]))
+        gather_in_two(v_g, v_pool, V_SPLIT)
 
         halves = NQ // P
-        p_t = sb.tile([P, PACK, NQ], F32)
+        pair = ps.tile([P, 2, P], F32, tag="bank4")
+        scores = []
         for h in range(halves):
             queries = slice(h * P, (h + 1) * P)
             for t in range(PACK):
-                score = ps.tile([P, P], F32, name="score", tag="bank%d" % (PACK * h + t))
+                if h == 1 and t < 2:
+                    score = pair[:, t, :]
+                else:
+                    score = ps.tile([P, P], F32, name="score", tag="bank%d" % (t + 3 * h))[:]
                 cols = slice(t * P, (t + 1) * P)
                 nc.tensor.matmul_mx(
-                    out=score[:],
+                    out=score,
                     lhsT=kw_g[:, cols].bitcast(FP8X4),
                     lhsT_scale=ks_g[:, cols],
                     rhs=qw[:, queries].bitcast(FP8X4),
@@ -97,7 +109,15 @@ def tile_attend_silu_kb_topkq256n512t1024_kernel(tc, q_words, q_scales, k_words,
                     start=True,
                     stop=True,
                 )
-                nc.scalar.activation(p_t[:, t, queries], score[:], ACT.Silu, bias=kb_col[:, t : t + 1])
+                scores.append(score)
+
+        p_t = sb.tile([P, PACK, NQ], F32)
+        for lo, hi in PIECES:
+            h = lo // P
+            for t in range(PACK):
+                nc.scalar.activation(
+                    p_t[:, t, lo:hi], scores[PACK * h + t][:, lo - h * P : hi - h * P], ACT.Silu, bias=kb_col[:, t : t + 1]
+                )
 
         v_t = ps.tile([P, 2, P], F32, tag="bank0")
         v_pairs = v_g[:].bitcast(F32)
@@ -106,35 +126,43 @@ def tile_attend_silu_kb_topkq256n512t1024_kernel(tc, q_words, q_scales, k_words,
         v_in = sb.tile([P, DV * PACK], BF16, align_bytes=64)
         nc.scalar.copy(v_in[:].bitcast(F32).rearrange("p (e u) -> p e u", u=2), v_t[:].rearrange("p u e -> p e u"))
 
-        w_in = []
-        for h in range(halves):
-            w_h = sb.tile([P, P, PACK], BF16, name="w_in%d" % h, align_bytes=64)
-            nc.vector.tensor_tensor(
-                w_h[:].rearrange("p (c i) t -> p c t i", i=2),
-                p_t[:, :, h * P : (h + 1) * P].rearrange("p t (c i) -> p c t i", i=2),
-                vs_col[:].unsqueeze(2).unsqueeze(1).to_broadcast([P, P // 2, PACK, 2]),
-                ALU.mult,
-            )
-            w_in.append(w_h)
-
+        w_in = sb.tile([P, NQ, PACK], BF16, align_bytes=64)
+        w_codes = sb.tile([P, NQ], U32, align_bytes=64)
+        w_scales = sb.tile([P, NQ], U8, align_bytes=64)
         v_codes = sb.tile([P, DV], U32, align_bytes=64)
         v_scales = sb.tile([P, DV], U8, align_bytes=64)
-        w_mx = []
-        for h in range(halves):
-            w_codes = sb.tile([P, P], U32, name="w_codes%d" % h, align_bytes=64)
-            w_scales = sb.tile([P, P], U8, name="w_scales%d" % h, align_bytes=64)
-            nc.vector.quantize_mx(out=w_codes[:].bitcast(FP8X4), scales=w_scales[:], in_=w_in[h][:].rearrange("p q t -> p (q t)"))
-            w_mx.append((w_codes, w_scales))
-            if h == 0:
-                nc.vector.quantize_mx(out=v_codes[:].bitcast(FP8X4), scales=v_scales[:], in_=v_in[:])
+
+        def product(engine, scale, lo, hi):
+            engine.tensor_tensor(
+                w_in[:, lo:hi, :].rearrange("p (c i) t -> p c t i", i=2),
+                p_t[:, :, lo:hi].rearrange("p t (c i) -> p c t i", i=2),
+                scale.unsqueeze(2).unsqueeze(1).to_broadcast([P, (hi - lo) // 2, PACK, 2]),
+                ALU.mult,
+            )
+
+        def quantise(lo, hi):
+            nc.vector.quantize_mx(
+                out=w_codes[:, lo:hi].bitcast(FP8X4),
+                scales=w_scales[:, lo:hi],
+                in_=w_in[:, lo:hi, :].rearrange("p q t -> p (q t)"),
+            )
+
+        vs_psum = vs_t[:, :, LIVE]
+        product(nc.vector, vs_psum, 0, 64)
+        product(nc.vector, vs_psum, 64, 128)
+        product(nc.vector, vs_psum, 128, 192)
+        quantise(0, 128)
+        product(nc.vector, vs_psum, 192, 256)
+        nc.vector.quantize_mx(out=v_codes[:].bitcast(FP8X4), scales=v_scales[:], in_=v_in[:])
+        quantise(128, 256)
 
         res = sb.tile([P, halves, DV], F32)
-        for h, (w_codes, w_scales) in enumerate(w_mx):
+        for h in range(halves):
             y = ps.tile([P, DV], F32, name="y%d" % h, tag="bank%d" % (h + 1))
             nc.tensor.matmul_mx(
                 out=y[:],
-                lhsT=w_codes[:].bitcast(FP8X4),
-                lhsT_scale=w_scales[:],
+                lhsT=w_codes[:, h * P : (h + 1) * P].bitcast(FP8X4),
+                lhsT_scale=w_scales[:, h * P : (h + 1) * P],
                 rhs=v_codes[:].bitcast(FP8X4),
                 rhs_scale=v_scales[:],
                 start=True,

@@ -17,7 +17,7 @@ P = 128
 PACK = 4
 LIVE = 127
 T, N, NQ, D, DV = 1024, 512, 256, 512, 128
-PIECES = [(0, 64),(64, 128),(128, 192),(192, 256)]
+PIECES = [(0, 128),(128, 256)]
 KB_SPLIT = 256
 V_SPLIT = 256
 FLOPS = 2 * D * N * NQ + 2 * N * NQ * DV
@@ -85,6 +85,8 @@ def tile_attend_silu_kb_topkq256n512t1024_kernel(tc, q_words, q_scales, k_words,
                 nc.tensor.transpose(turned[:, t, :], row[:, t:N:PACK], ident32[:])
         kb_col = sb.tile([P, PACK], F32)
         nc.scalar.copy(kb_col[:], kb_t[:, :, LIVE])
+        vs_col = sb.tile([P, PACK], F32)
+        nc.scalar.copy(vs_col[:], vs_t[:, :, LIVE])
 
         v_g = sb.tile([P, N], BF16, align_bytes=64)
         gather_in_two(v_g, v_pool, V_SPLIT)
@@ -148,11 +150,10 @@ def tile_attend_silu_kb_topkq256n512t1024_kernel(tc, q_words, q_scales, k_words,
             )
 
         vs_psum = vs_t[:, :, LIVE]
-        product(nc.vector, vs_psum, 0, 64)
-        product(nc.vector, vs_psum, 64, 128)
-        product(nc.vector, vs_psum, 128, 192)
+        product(nc.vector, vs_psum, 0, 128)
+        product(nc.vector, vs_psum, 128, 224)
+        product(nc.gpsimd, vs_col[:], 224, 256)
         quantise(0, 128)
-        product(nc.vector, vs_psum, 192, 256)
         nc.vector.quantize_mx(out=v_codes[:].bitcast(FP8X4), scales=v_scales[:], in_=v_in[:])
         quantise(128, 256)
 

@@ -19,7 +19,6 @@ LIVE = 127
 T, N, NQ, D, DV = 1024, 512, 256, 512, 128
 PIECES = [(0, 128),(128, 256)]
 KB_SPLIT = 256
-V_SPLIT = 256
 FLOPS = 2 * D * N * NQ + 2 * N * NQ * DV
 
 
@@ -31,6 +30,7 @@ def tile_attend_silu_kb_topkq256n512t1024_kernel(tc, q_words, q_scales, k_words,
     nc = tc.nc
     with ExitStack() as ctx:
         sb = ctx.enter_context(tc.tile_pool(name="sb", bufs=1))
+        shared = ctx.enter_context(tc.tile_pool(name="shared", bufs=1))
         ps = ctx.enter_context(tc.psum_pool(name="ps", bufs=1))
 
         offsets = sb.tile([P, N // 16], U16)
@@ -38,7 +38,7 @@ def tile_attend_silu_kb_topkq256n512t1024_kernel(tc, q_words, q_scales, k_words,
         vs_pool = sb.tile([P, T], F32)
         ks_pool = sb.tile([P, T], U8, align_bytes=64)
         kw_pool = sb.tile([P, T], I32, align_bytes=64)
-        v_pool = sb.tile([P, T], F32)
+        v_pool = shared.tile([P, T], F32, offset=0, align_bytes=64)
         qw = sb.tile([P, NQ], I32, align_bytes=64)
         qs = sb.tile([P, NQ], U8, align_bytes=64)
         ident32 = sb.tile([P, P], F32)
@@ -60,10 +60,10 @@ def tile_attend_silu_kb_topkq256n512t1024_kernel(tc, q_words, q_scales, k_words,
             nc.sync.dma_start(ks_pool[f:P:32, :].bitcast(I32), k_scales[0, f:16:4, :].bitcast(I32))
         nc.sync.dma_start(vs_pool[LIVE:P, :], vs[LIVE:P, :])
         nc.sync.dma_start(kw_pool[:], k_words[0].rearrange("p n r -> p (n r)").bitcast(I32))
-        nc.sync.dma_start(v_pool[:], vT)
         nc.sync.dma_start(qw[:], q_words[0, 0].rearrange("p n r -> p (n r)").bitcast(I32))
         for f in range(4):
             nc.sync.dma_start(qs[f:P:32, :].bitcast(I32), q_scales[0, 0, f:16:4, :].bitcast(I32))
+        nc.sync.dma_start(v_pool[:], vT)
 
         def gather_in_two(dst, pool, split):
             nc.vector.tensor_copy(dst[:, :split], pool[:].indirect(offsets[:, : split // 16]))
@@ -89,7 +89,7 @@ def tile_attend_silu_kb_topkq256n512t1024_kernel(tc, q_words, q_scales, k_words,
         nc.scalar.copy(vs_col[:], vs_t[:, :, LIVE])
 
         v_g = sb.tile([P, N], BF16, align_bytes=64)
-        gather_in_two(v_g, v_pool, V_SPLIT)
+        nc.vector.tensor_copy(v_g[:], v_pool[:].indirect(offsets[:]))
 
         halves = NQ // P
         pair = ps.tile([P, 2, P], F32, tag="bank4")
@@ -128,7 +128,7 @@ def tile_attend_silu_kb_topkq256n512t1024_kernel(tc, q_words, q_scales, k_words,
         v_in = sb.tile([P, DV * PACK], BF16, align_bytes=64)
         nc.scalar.copy(v_in[:].bitcast(F32).rearrange("p (e u) -> p e u", u=2), v_t[:].rearrange("p u e -> p e u"))
 
-        w_in = sb.tile([P, NQ, PACK], BF16, align_bytes=64)
+        w_in = shared.tile([P, NQ, PACK], BF16, offset=0, align_bytes=64)
         w_codes = sb.tile([P, NQ], U32, align_bytes=64)
         w_scales = sb.tile([P, NQ], U8, align_bytes=64)
         v_codes = sb.tile([P, DV], U32, align_bytes=64)

@@ -34,7 +34,7 @@ def tile_attend_silu_kb_topkq256n512t1024_kernel(tc, q_words, q_scales, k_words,
         ps = ctx.enter_context(tc.psum_pool(name="ps", bufs=1))
 
         offsets = sb.tile([P, N // 16], U16)
-        kb_pool = sb.tile([P, T], F32)
+        kb_pool = shared.tile([P, T], F32, offset=4096, align_bytes=64)
         vs_pool = sb.tile([P, T], F32)
         ks_pool = sb.tile([P, T], U8, align_bytes=64)
         kw_pool = sb.tile([P, T], I32, align_bytes=64)
@@ -43,6 +43,8 @@ def tile_attend_silu_kb_topkq256n512t1024_kernel(tc, q_words, q_scales, k_words,
         qs = sb.tile([P, NQ], U8, align_bytes=64)
         ident32 = sb.tile([P, P], F32)
 
+        nc.sync.dma_start(offsets[:], offs)
+        nc.scalar.dma_start(vs_pool[LIVE:P, :], vs[LIVE:P, :])
         nc.vector.memset(ks_pool[:].bitcast(I32), 0)
         warm_in = sb.tile([P, 8], F32)
         nc.vector.memset(warm_in[:], 0.0)
@@ -54,11 +56,9 @@ def tile_attend_silu_kb_topkq256n512t1024_kernel(tc, q_words, q_scales, k_words,
         make_identity(nc, ident32[:], nomemset=True)
         nc.vector.memset(vs_pool[0:LIVE, :], 0.0)
 
-        nc.sync.dma_start(offsets[:], offs)
         nc.sync.dma_start(kb_pool[LIVE:P, :], kb[LIVE:P, :])
         for f in range(4):
             nc.sync.dma_start(ks_pool[f:P:32, :].bitcast(I32), k_scales[0, f:16:4, :].bitcast(I32))
-        nc.sync.dma_start(vs_pool[LIVE:P, :], vs[LIVE:P, :])
         nc.sync.dma_start(kw_pool[:], k_words[0].rearrange("p n r -> p (n r)").bitcast(I32))
         nc.sync.dma_start(qw[:], q_words[0, 0].rearrange("p n r -> p (n r)").bitcast(I32))
         for f in range(4):
@@ -71,7 +71,7 @@ def tile_attend_silu_kb_topkq256n512t1024_kernel(tc, q_words, q_scales, k_words,
 
         kb_g = sb.tile([P, N], F32)
         gather_in_two(kb_g, kb_pool, KB_SPLIT)
-        vs_g = sb.tile([P, N], F32)
+        vs_g = shared.tile([P, N], F32, offset=4096, align_bytes=64)
         nc.scalar.activation(vs_g[:], vs_pool[:].indirect(offsets[:]), ACT.Copy)
         ks_g = sb.tile([P, N], U8, align_bytes=64)
         nc.vector.tensor_copy(by_place(ks_g[:]), ks_pool[:].indirect(offsets[:]))

from contextlib import ExitStack

import concourse.mybir as mybir
from concourse.masks import make_identity

F32 = mybir.dt.float32
BF16 = mybir.dt.bfloat16
I32 = mybir.dt.int32
U32 = mybir.dt.uint32
U16 = mybir.dt.uint16
U8 = mybir.dt.uint8
FP8X4 = mybir.dt.float8_e4m3fn_x4
ACT = mybir.ActivationFunctionType
ALU = mybir.AluOpType

P = 128
PACK = 4
LIVE = 127
T, N, NQ, D, DV = 1024, 512, 256, 512, 128
PIECES = [(0, 128),(128, 256)]
KB_SPLIT = 256
FLOPS = 2 * D * N * NQ + 2 * N * NQ * DV


def by_place(tile):
    return tile.rearrange("p (t s) -> p s t", t=PACK)


def tile_attend_silu_kb_topkq256n512t1024_kernel(tc, q_words, q_scales, k_words, k_scales, vT, vs, kb, offs, out):
    nc = tc.nc
    with ExitStack() as ctx:
        sb = ctx.enter_context(tc.tile_pool(name="sb", bufs=1))
        shared = ctx.enter_context(tc.tile_pool(name="shared", bufs=1))
        ps = ctx.enter_context(tc.psum_pool(name="ps", bufs=1))

        offsets = sb.tile([P, N // 16], U16)
        kb_pool = shared.tile([P, T], F32, offset=4096, align_bytes=64)
        vs_pool = sb.tile([P, T], F32)
        ks_pool = sb.tile([P, T], U8, align_bytes=64)
        kw_pool = sb.tile([P, T], I32, align_bytes=64)
        v_pool = shared.tile([P, T], F32, offset=0, align_bytes=64)
        qw = sb.tile([P, NQ], I32, align_bytes=64)
        qs = sb.tile([P, NQ], U8, align_bytes=64)
        ident32 = sb.tile([P, P], F32)

        nc.sync.dma_start(offsets[:], offs)
        nc.scalar.dma_start(vs_pool[LIVE:P, :], vs[LIVE:P, :])
        nc.vector.memset(ks_pool[:].bitcast(I32), 0)
        warm_in = sb.tile([P, 8], F32)
        nc.vector.memset(warm_in[:], 0.0)
        warm_out = sb.tile([P, 8], F32)
        nc.scalar.activation(warm_out[:], warm_in[:], ACT.Silu)
        nc.vector.memset(kb_pool[0:LIVE, :], 0.0)
        nc.vector.memset(qs[:].bitcast(I32), 0)
        nc.vector.memset(ident32[:], 0.0)
        make_identity(nc, ident32[:], nomemset=True)
        nc.vector.memset(vs_pool[0:LIVE, :], 0.0)

        nc.sync.dma_start(kb_pool[LIVE:P, :], kb[LIVE:P, :])
        for f in range(4):
            nc.sync.dma_start(ks_pool[f:P:32, :].bitcast(I32), k_scales[0, f:16:4, :].bitcast(I32))
        nc.sync.dma_start(kw_pool[:], k_words[0].rearrange("p n r -> p (n r)").bitcast(I32))
        nc.sync.dma_start(qw[:], q_words[0, 0].rearrange("p n r -> p (n r)").bitcast(I32))
        for f in range(4):
            nc.sync.dma_start(qs[f:P:32, :].bitcast(I32), q_scales[0, 0, f:16:4, :].bitcast(I32))
        nc.sync.dma_start(v_pool[:], vT)

        def gather_in_two(dst, pool, split):
            nc.vector.tensor_copy(dst[:, :split], pool[:].indirect(offsets[:, : split // 16]))
            nc.scalar.activation(dst[:, split:], pool[:].indirect(offsets[:, split // 16 :]), ACT.Copy)

        kb_g = sb.tile([P, N], F32)
        gather_in_two(kb_g, kb_pool, KB_SPLIT)
        vs_g = shared.tile([P, N], F32, offset=4096, align_bytes=64)
        nc.scalar.activation(vs_g[:], vs_pool[:].indirect(offsets[:]), ACT.Copy)
        ks_g = sb.tile([P, N], U8, align_bytes=64)
        nc.vector.tensor_copy(by_place(ks_g[:]), ks_pool[:].indirect(offsets[:]))
        kw_g = sb.tile([P, N], U32, align_bytes=64)
        nc.vector.tensor_copy(by_place(kw_g[:]), kw_pool[:].bitcast(U32).indirect(offsets[:]))

        kb_t = ps.tile([P, PACK, P], F32, tag="bank6")
        vs_t = ps.tile([P, PACK, P], F32, tag="bank7")
        for turned, row in ((kb_t, kb_g), (vs_t, vs_g)):
            for t in range(PACK):
                nc.tensor.transpose(turned[:, t, :], row[:, t:N:PACK], ident32[:])
        kb_col = sb.tile([P, PACK], F32)
        nc.scalar.copy(kb_col[:], kb_t[:, :, LIVE])
        vs_col = sb.tile([P, PACK], F32)
        nc.scalar.copy(vs_col[:], vs_t[:, :, LIVE])

        v_g = sb.tile([P, N], BF16, align_bytes=64)
        nc.vector.tensor_copy(v_g[:], v_pool[:].indirect(offsets[:]))

        halves = NQ // P
        pair = ps.tile([P, 2, P], F32, tag="bank4")
        scores = []
        for h in range(halves):
            queries = slice(h * P, (h + 1) * P)
            for t in range(PACK):
                if h == 1 and t < 2:
                    score = pair[:, t, :]
                else:
                    score = ps.tile([P, P], F32, name="score", tag="bank%d" % (t + 3 * h))[:]
                cols = slice(t * P, (t + 1) * P)
                nc.tensor.matmul_mx(
                    out=score,
                    lhsT=kw_g[:, cols].bitcast(FP8X4),
                    lhsT_scale=ks_g[:, cols],
                    rhs=qw[:, queries].bitcast(FP8X4),
                    rhs_scale=qs[:, queries],
                    start=True,
                    stop=True,
                )
                scores.append(score)

        p_t = sb.tile([P, PACK, NQ], F32)
        for lo, hi in PIECES:
            h = lo // P
            for t in range(PACK):
                nc.scalar.activation(
                    p_t[:, t, lo:hi], scores[PACK * h + t][:, lo - h * P : hi - h * P], ACT.Silu, bias=kb_col[:, t : t + 1]
                )

        v_t = ps.tile([P, 2, P], F32, tag="bank0")
        v_pairs = v_g[:].bitcast(F32)
        for u in range(2):
            nc.tensor.transpose(v_t[:, u, :], v_pairs[:, u : N // 2 : 2], ident32[:])
        v_in = sb.tile([P, DV * PACK], BF16, align_bytes=64)
        nc.scalar.copy(v_in[:].bitcast(F32).rearrange("p (e u) -> p e u", u=2), v_t[:].rearrange("p u e -> p e u"))

        w_in = shared.tile([P, NQ, PACK], BF16, offset=0, align_bytes=64)
        w_codes = sb.tile([P, NQ], U32, align_bytes=64)
        w_scales = sb.tile([P, NQ], U8, align_bytes=64)
        v_codes = sb.tile([P, DV], U32, align_bytes=64)
        v_scales = sb.tile([P, DV], U8, align_bytes=64)

        def product(engine, scale, lo, hi):
            engine.tensor_tensor(
                w_in[:, lo:hi, :].rearrange("p (c i) t -> p c t i", i=2),
                p_t[:, :, lo:hi].rearrange("p t (c i) -> p c t i", i=2),
                scale.unsqueeze(2).unsqueeze(1).to_broadcast([P, (hi - lo) // 2, PACK, 2]),
                ALU.mult,
            )

        def quantise(lo, hi):
            nc.vector.quantize_mx(
                out=w_codes[:, lo:hi].bitcast(FP8X4),
                scales=w_scales[:, lo:hi],
                in_=w_in[:, lo:hi, :].rearrange("p q t -> p (q t)"),
            )

        vs_psum = vs_t[:, :, LIVE]
        product(nc.vector, vs_psum, 0, 128)
        product(nc.vector, vs_psum, 128, 224)
        product(nc.gpsimd, vs_col[:], 224, 256)
        quantise(0, 128)
        nc.vector.quantize_mx(out=v_codes[:].bitcast(FP8X4), scales=v_scales[:], in_=v_in[:])
        quantise(128, 256)

        res = sb.tile([P, halves, DV], F32)
        for h in range(halves):
            y = ps.tile([P, DV], F32, name="y%d" % h, tag="bank%d" % (h + 1))
            nc.tensor.matmul_mx(
                out=y[:],
                lhsT=w_codes[:, h * P : (h + 1) * P].bitcast(FP8X4),
                lhsT_scale=w_scales[:, h * P : (h + 1) * P],
                rhs=v_codes[:].bitcast(FP8X4),
                rhs_scale=v_scales[:],
                start=True,
                stop=True,
            )
            if h == 0:
                nc.scalar.activation(res[:, h, :], y[:], ACT.Copy, scale=1.0 / 16.0)
            else:
                nc.vector.tensor_scalar(res[:, h, :], y[:], 1.0 / 16.0, None, ALU.mult)
            nc.sync.dma_start(out[0, h * P : (h + 1) * P, :], res[:, h, :])
